import numpy as np, ml_dtypes
CORES = [3,11,19,27,35,43,51,59]
N = 8
BF = ml_dtypes.bfloat16
def gentries(a):
    return np.ascontiguousarray(a.reshape(8, 16, -1).transpose(0, 2, 1)).reshape(8, -1)
def gtable(e):
    e = np.asarray(e); return np.ascontiguousarray(e.reshape(8, -1, 16).transpose(0, 2, 1)).reshape(128, -1).astype(np.int32)
W, S, L, RO, RW, BC, BR = 3072, 12, 256, 3, 3, 2, 2
def people(rng, street, fame, one):
    sh = (N, 8, 16, W); col = np.arange(W) % S
    a = np.where(rng.random(sh) < street, S * rng.integers(0, L, sh) + col, rng.integers(0, W, sh))
    st = rng.integers(0, L, (N * 8, 24)); star = S * np.take_along_axis(st, rng.integers(0, 24, (N * 8, 16 * W)), 1).reshape(sh) + col
    a = np.where(rng.random(sh) < fame, star, a)
    return np.where(rng.random((N, 8, 1, W)) < one, a[:, :, :1], a)
def strangers(rng, *sh):
    return S * rng.integers(0, L, sh + (W,)) + (np.arange(W) + rng.integers(1, S, sh + (W,))) % S
def pack(x, a, tt):
    return {"x": np.ascontiguousarray(np.reshape(x, (N, 128, W))).astype(np.float32).astype(BF), "aq": np.ascontiguousarray(np.reshape(a, (N, 128, W))).astype(np.int32),
            "tg": np.stack([gtable(b) for b in tt])}
def mixed(rng):
    return people(rng, rng.choice(np.array([0.3, 0.5, 0.7]), (N, 8, 1, 1)), rng.choice(np.array([0.0, 0.05, 0.15]), (N, 8, 1, 1)), 0.02)
def setup_inputs(rng):
    return pack(rng.integers(0, 256, (N, 8, 16, W)), mixed(rng), rng.integers(0, W, (N, 8, W)))
def setup_inputs_ties(rng):
    x = 127 * rng.integers(0, 3, (N, 8, 16, W)); a = mixed(rng)
    x[:, 0] = 255 * rng.integers(0, 2, (N, 1, W)); x[:, 1] = rng.integers(0, 2, (N, 16, W)); x[:, 3] = rng.integers(0, 256, (N, 16, 1))
    x[:, 5] = rng.integers(0, 256, (16, 4))[:, rng.integers(0, 4, (N, W))].transpose(1, 0, 2)
    a[:, 6, 8:] = a[:, 6, :8]; a[:, 7, 1:] = a[:, 7, :15]
    return pack(x, a, rng.integers(0, W, (N, 8, W)))
def setup_inputs_stars(rng):
    a = np.zeros((N, 8, 16, W), np.int64); ev = a[:, ::2].shape
    a[:, ::2] = S * rng.choice(np.array([0, 1, 2, 3, 4, 5, L - 8, L - 1]), ev) + np.arange(W) % S
    a[:, 1::2] = rng.choice(np.array([0, 1, W // 2, W - 2, W - 1]), ev)
    a = np.where(rng.random((N, 8, 1, W)) < 0.2, a[:, :, :1], a)
    return pack(rng.integers(0, 256, (N, 8, 16, W)), a, rng.choice(np.array([0, 1, W // 2, W - 2, W - 1, W // 4]), (N, 8, W)))
def setup_inputs_free(rng):
    a = mixed(rng); a[:, ::2] = strangers(rng, N, 4, 16)
    x = rng.integers(0, 256, (N, 8, 16, W)); x[:, :4] = x[:, :4] & 1; x[:, 4:6] = x[:, 4:6] & 63
    share = np.zeros((N, 6, 1, 1)); share[1::2, :2] = 1.0; share[:, 2:4] = 0.5; share[:, 4:6] = 0.03
    x[:, :6] = np.where(rng.random((N, 6, 1, W)) < share, 255 - x[:, :6], x[:, :6])
    return pack(x, a, rng.integers(0, W, (N, 8, W)))
def setup_inputs_chains(rng):
    a = mixed(rng); a[:, ::2] = strangers(rng, N, 4, 16)
    i = np.arange(L); bl = i[(i % 8 > RW) & (i % 8 <= RW + BC)]; n = len(bl)
    for q in range(N):
        for g in range(8):
            for t in range(RO):
                o = rng.permutation(bl); c = rng.integers(0, 6, n)
                nx = np.where(c == 0, rng.integers(0, L, n), np.where(c == 1, o, np.roll(o, -1)))
                nx[0] = o[0]; nx[1] = o[2]; nx[2] = o[1]; nx[3:10] = o[4:11]
                town = a[q, g]; town[:, S * o + t] = S * nx + t
    return pack(rng.integers(0, 256, (N, 8, 16, W)), a, rng.integers(0, W, (N, 8, W)))
def setup_inputs_spread(rng):
    x = np.minimum((np.exp2(8 * rng.random((N, 8, 1, W))) * rng.random((N, 8, 16, W))).astype(np.int64), 255)
    e = rng.choice(np.array([1.0, 2.0, 4.0]), (N, 8, 1, 1)); sh = (N, 8, 16, W)
    a = np.minimum((W * np.power(rng.random(sh), e)).astype(np.int64), W - 1)
    s = S * np.minimum((L * np.power(rng.random(sh), e)).astype(np.int64), L - 1) + np.arange(W) % S
    a = np.where(rng.random(sh) < rng.random((N, 8, 1, 1)), s, a)
    return pack(x, a, np.minimum((W * np.power(rng.random((N, 8, W)), e[:, :, 0])).astype(np.int64), W - 1))
def check_inputs(d):
    bad = []; xf = np.asarray(d["x"]).astype(np.float32)
    if not np.all((xf >= 0) & (xf <= 255) & (xf == np.floor(xf))): bad.append("whole numbers and range of x")
    for k in ("aq", "tg"):
        if np.min(d[k]) < 0 or np.max(d[k]) > W - 1: bad.append("range of " + k)
    return bad
def reference(x, aq, tg):
    xs = x.astype(np.float32).astype(np.int32).reshape(N, 8, 16, W); aw = aq.astype(np.int64).reshape(N, 8, 16, W)
    tt = np.stack([gentries(a) for a in tg]).astype(np.int64)
    lane = np.arange(L); role = lane % 8; ri = np.arange(N)[:, None]; gi = np.arange(8)[None, :]
    blk = (role > RW) & (role <= RW + BC)
    yx = np.zeros((N, 8, 16, RO, L), np.float32); ym = np.zeros((N, 8, RO, L), np.float32)
    for t in range(RO):
        v = S * lane + t; xv = xs[..., v]; own = aw[..., v]
        near = np.take_along_axis(xs, own.reshape(N, 8, 1, 16 * L), 3).reshape(N, 8, 16, 16, L)
        c = np.add.reduce(np.abs(near - xv[:, :, :, None, :]), axis=2); k = np.argmax(c, axis=2)
        tt[:, :, v] = np.take_along_axis(own, k[:, :, None, :], 2)[:, :, 0]
        uu = np.take_along_axis(own, ((k + 1) % 16)[:, :, None, :], 2)[:, :, 0]
        p = tt[:, :, v][..., 0::8]; o = uu[..., 0::8]; D = p.shape[-1]
        meet = (p[..., None] == p[:, :, None, :]) | (p[..., None] == o[:, :, None, :]) | (o[..., None] == p[:, :, None, :]) | (o[..., None] == o[:, :, None, :])
        void = (p == o) | np.any(meet & (np.tri(D, D, -1) > 0), axis=-1)
        s = np.zeros((N, 8, W), np.int64) + np.arange(W)
        q, g, i = np.nonzero(~void); s[q, g, p[q, g, i]] = o[q, g, i]; s[q, g, o[q, g, i]] = p[q, g, i]
        tt = np.take_along_axis(s, tt, 2); uu = np.take_along_axis(s, uu, 2)
        for w in range(1, RW + 1):
            place = tt[:, :, v][..., w::8]; val = uu[..., w::8]
            for i in range(place.shape[-1] - 1, -1, -1):
                tt[ri, gi, place[..., i]] = val[..., i]
        tv = tt[:, :, v]; bt = tv[..., blk]; b = np.zeros((N, 8, W), bool)
        for rnd in range(BR):
            q, g, i = np.nonzero(~b[:, :, v[blk]]); b = np.zeros((N, 8, W), bool); b[q, g, bt[q, g, i]] = True
        free = ~b[:, :, v]
        nx = []; nm = []
        for r in range(N):
            h = (r + 1 + t % (N - 1)) % N; a = tv[r]
            al = np.take_along_axis(aw[h], a[:, None, :], 2)
            far = np.take_along_axis(xs[h], al.reshape(8, 1, 16 * L), 2).reshape(8, 16, 16, L)
            e = np.add.reduce(np.abs(far - xv[r][:, :, None, :]), axis=1); k = np.argmin(e, axis=1)
            m = np.take_along_axis(al, k[:, None, :], 1)[:, 0]; xa = np.take_along_axis(xs[h], a[:, None, :], 2)
            nx.append(np.where(free[r][:, None, :], (xv[r] + xa) >> 1, xv[r])); nm.append(np.where(free[r], m, own[r, :, t]))
        nx = np.stack(nx); nm = np.stack(nm)
        xs[..., v] = nx; aw[:, :, t, v] = nm; yx[:, :, :, t] = nx; ym[:, :, t] = nm
    return {"yx": yx.reshape(N, 128, RO * L).astype(BF), "ym": ym.reshape(N, 8, RO * L).astype(np.float32), "yt": tt.astype(np.float32)}

from concourse.mybir import AluOpType, ActivationFunctionType

ALU = AluOpType
ACT = ActivationFunctionType
W, L, NT, ST = 3072, 256, 3, 12
F, B, I, U, H = "float32", "bfloat16", "int32", "uint16", "float16"
BIG = 10000.0
VJ = (4, 5, 6)


def _sb(n, d):
    return ("sbuf", [128, n], d)


SCRATCH = {
    "X": _sb(W, B), "XH": _sb(W, B), "AQ": _sb(W, I), "TG": _sb(192, I), "TG16": _sb(192, U),
    "SS": _sb(W + 64, F), "ID": _sb(W, F), "TT": _sb(2 * W + 32, F), "YT": _sb(2 * W + 32, F),
    "ip": _sb(8, I), "iq": _sb(8, I), "col": _sb(16, F), "i144": _sb(144, I), "ik": _sb(128, I), "ig": _sb(128, I),
    "W1": _sb(144, B), "W2": _sb(144, B), "Wn": _sb(144, B), "Wh": _sb(144, H),
    "BO": _sb(128, B), "Ib": _sb(128, B), "In": _sb(128, B), "DT": _sb(128, F), "DU": _sb(128, F), "t1": _sb(128, F), "t2": _sb(128, F),
    "t4": _sb(128, F), "E": _sb(2048, B), "MS": _sb(256, F), "MM": _sb(256, F), "MR": _sb(256, F), "ia": _sb(256, I), "t3": _sb(256, F),
    "isw": _sb(128, I), "OFW": _sb(72, F), "MW": _sb(72, F), "OFD": _sb(264, F), "MD": _sb(264, F), "MB": _sb(256, F),
    "il": _sb(18, I), "il2": _sb(24, I), "il3": _sb(16, I), "CT": _sb(16, U), "LH": _sb(24, U), "LD": _sb(54, U), "LX": _sb(48, U),
    "MK": _sb(16, F), "DM": _sb(8, F), "BID": _sb(8, F), "LID": _sb(768, F), "MT": _sb(8, F),
    "XN": _sb(768, B), "XV": _sb(768, B), "XO": _sb(256, B), "XF": _sb(256, F), "XT": _sb(384, B),
    "XRo": _sb(2048, B), "XR1": _sb(2048, B), "XR2": _sb(2048, B),
    "OF": _sb(256, U), "OF1": _sb(256, U), "OF2": _sb(256, U), "AL": _sb(256, U), "ALf": _sb(256, F), "ALT": _sb(256, F),
    "GA": _sb(2048, B), "GB": _sb(2048, B), "HA": _sb(2048, B), "HB": _sb(2048, B), "AD": _sb(2048, B), "MX": _sb(2048, B),
    "DUP": _sb(288, F), "DUQ": _sb(288, F), "X2": _sb(768, F), "X3": _sb(768, F), "DTU": _sb(384, F),
    "R": _sb(256, F), "NR": _sb(256, F), "SC": _sb(384, F), "UT": _sb(72, U), "OP": _sb(4, U), "RAW": _sb(64, F),
    "EQ": _sb(264, F), "FL": _sb(264, F), "O6": _sb(24, U), "UR": _sb(288, F), "ZC": _sb(32, F), "EW": _sb(72, F), "FW": _sb(72, F),
    "OW": _sb(18, U), "AS": _sb(256, F), "RQ": _sb(48, U), "RI": _sb(48, U), "DD": _sb(768, H), "DI": _sb(768, H),
    "BT": _sb(64, F), "BC": _sb(64, F), "EB": _sb(256, F), "FB": _sb(256, F), "EL": _sb(1024, B), "Ab": _sb(256, B), "FM": _sb(768, F),
    "Y": _sb(256, F), "YX": _sb(768, B), "YM": _sb(768, F), "RM": _sb(256, F), "k1": _sb(16, I), "k2": _sb(16, I), "KL": _sb(16, U),
    "MP": _sb(256, H), "ML": _sb(48, U), "MI": _sb(48, U), "d1": _sb(256, F), "KP": _sb(256, F), "NF": _sb(256, F),
    "RR": _sb(512, F), "SW": _sb(64, F),
    "D1": ("psum", [128, 512], F), "D2": ("psum", [128, 512], F), "PA": ("psum", [128, 512], F), "PB": ("psum", [128, 512], F),
    "r0": ("psum", [128, 512], F), "r1": ("psum", [128, 512], F), "r2": ("psum", [128, 512], F), "r3": ("psum", [128, 512], F),
}
SEMAPHORES = ["sV", "sS", "sP", "sG", "lx", "la0", "la1", "lt", "lh", "sent", "ox", "om", "ot"] + \
    [a + str(t) for a in ("xv", "rq", "dd", "mm") for t in range(NT)]
PSUM = ("D1", "D2", "PA", "PB", "r0", "r1", "r2", "r3")


def rank_program(g, core, T, topo):
    rank = T.rank_of(core)
    if rank is None:
        return
    N = len(T.cores)
    Q = {"V": g.vector, "S": g.scalar, "P": g.tensor, "G": g, "Y": g.sync}
    cnt = {}
    known = {e: {} for e in Q}
    clock, wr, rd, part = {}, {}, {}, {}

    def need(e, ev):
        s, n = ev
        if known[e].get(s, 0) >= n:
            return
        Q[e].wait_ge(T.sem[s], n)
        known[e][s] = n
        for k, x in clock.get(ev, {}).items():
            if known[e].get(k, 0) < x:
                known[e][k] = x

    def sync(e, r, w):
        own = "s" + e
        evs = []
        for a in r:
            if a in wr:
                evs.append(wr[a])
            if a in PSUM:
                evs += [x for x in rd.get(a, []) if x[0] != own]
        for a in w:
            if a[0] == "+":
                a = a[1:]
                if part.get(a) == e and not rd.get(a):
                    continue
            evs += rd.get(a, []) + ([wr[a]] if a in wr else [])
        best = {}
        for s, n in evs:
            if not (e == "P" and s == own):
                best[s] = max(best.get(s, 0), n)
        for s in sorted(best):
            need(e, (s, best[s]))

    def done(e, ev, r, w):
        clock[ev] = dict(known[e])
        for a in r:
            rd.setdefault(a, []).append(ev)
        for a in w:
            n = a.lstrip("+")
            wr[n] = ev
            rd[n] = []
            part[n] = e if a[0] == "+" else None

    def op(e, fn, r, w):
        r, w = r.split(), w.split()
        sync(e, r, w)
        s = "s" + e
        cnt[s] = cnt.get(s, 0) + 1
        fn().then_inc(T.sem[s], 1)
        done(e, (s, cnt[s]), r, w)

    def dma(e, s, out, in_, r, w):
        r, w = r.split(), w.split()
        sync(e, r, w)
        cnt[s] = cnt.get(s, 0) + 16
        Q[e].dma_start(out, in_).then_inc(T.sem[s], 16)
        done(e, (s, cnt[s]), r, w)

    def send(dst, s, out, in_, r):
        sync("G", r.split(), [])
        rid, pid, _e = topo.addr(dst)
        g.remote_dma(out, in_, T.sem[s], T.sem.sent, pid, rid, topo.mask(core, dst))
        cnt["sent"] = cnt.get("sent", 0) + len(topo.engines(core, dst))

    def arrive(src, s, w):
        cnt[s] = len(topo.engines(src, core))
        wr[w] = (s, cnt[s])

    v, sc, pe = g.vector, g.scalar, g.tensor

    def cp(out, in_, r, w):
        op("V", lambda: v.tensor_copy(out, in_), r, w)

    def tt(out, a, b, o, r, w):
        op("V", lambda: v.tensor_tensor(out, a, b, o), r, w)

    def ts(out, a, s1, o1, r, w, s2=None, o2=None):
        if o2 is None:
            op("V", lambda: v.tensor_scalar(out, a, s1, None, o1), r, w)
        else:
            op("V", lambda: v.tensor_scalar(out, a, s1, s2, o1, o2), r, w)

    def scan(out, a, b, ini, o0, o1, r, w):
        op("V", lambda: v.tensor_tensor_scan(out, a, b, ini, o0, o1), r, w)

    def ms(out, c, w):
        op("V", lambda: v.memset(out, c), "", w)

    def tr(out, in_, r, w):
        op("V", lambda: v.transpose(out, in_), r, w)

    def act(out, in_, f, r, w, **k):
        op("S", lambda: sc.activation(out, in_, f, **k), r, w)

    def mm(out, a, b, st, sp, r, w):
        op("P", lambda: pe.matmul(out, a, b, st, sp), r, w)

    def iota(out, pat, base, cm, w, small=False):
        if small:
            op("G", lambda: g.iota(out, pat, base, cm, allow_small_or_imprecise_dtypes=True), "", w)
        else:
            op("G", lambda: g.iota(out, pat, base, cm), "", w)

    host = [T.cores[(rank + 1 + t % (N - 1)) % N] for t in range(NT)]
    guest = [T.cores[(rank - 1 - t % (N - 1)) % N] for t in range(NT)]
    for t in range(NT):
        arrive(guest[t], "xv%d" % t, "XV%d" % t)
        arrive(guest[t], "rq%d" % t, "RI%d" % t)
        arrive(host[t], "dd%d" % t, "DI%d" % t)
        arrive(host[t], "mm%d" % t, "MI%d" % t)
    XR = [None, T.XR1, T.XR2]
    OF = [T.OF, T.OF1, T.OF2]
    AQ = "AQ0 AQ1"

    dma("Y", "lx", T.X[:], T.x[:], "", "X")
    for h in range(2):
        for c in range(2):
            a = 1536 * c + 768 * h
            dma("Y", "la%d" % h, T.AQ[:, a:a + 768], T.aq[:, a:a + 768], "", "+AQ%d" % h)
    dma("Y", "lt", T.TG[:], T.tg[:], "", "TG")

    iota(T.ip[:], [[0, 8]], 0, 1, "ip")
    iota(T.i144[:], [[1, 144]], 0, 0, "i144")
    iota(T.il3[:], [[192, 2], [384, 4], [96, 2]], 0, 0, "il3")
    iota(T.ig[:], [[1, 8], [0, 16]], 0, 0, "ig")
    iota(T.ik[:], [[0, 8], [1, 16]], 0, 0, "ik")
    iota(T.il[:, 0:16], [[12, 8], [1536, 2]], 0, 0, "+il")
    iota(T.il[:, 16:18], [[0, 2]], 0, 0, "+il")
    iota(T.ia[:], [[0, 16], [1, 16]], 0, 0, "ia")
    iota(T.isw[:], [[0, 4], [1, 32]], 0, 0, "isw")
    iota(T.OFD[:], [[0, 264]], 0, 0, "OFD", True)
    iota(T.OFW[:], [[0, 72]], 0, 0, "OFW", True)
    ts(T.iq[:, 0:1], T.ip[:, 0:1], 15, ALU.bitwise_and, "ip", "iq0")
    ts(T.iq[:, 1:2], T.ip[:, 0:1], 4, ALU.arith_shift_right, "ip", "iq1")
    ts(T.iq[:, 2:3], T.ip[:, 0:1], 31, ALU.bitwise_and, "ip", "iq2")
    ts(T.iq[:, 3:4], T.ip[:, 0:1], 1, ALU.bitwise_and, "ip", "iq3")
    ts(T.iq[:, 4:5], T.ip[:, 0:1], 16, ALU.bitwise_and, "ip", "iq4")
    cp(T.col[:, 0:1], T.ip[:, 0:1], "ip", "c0")
    cp(T.col[:, 1:4], T.iq[:, 0:3], "iq0 iq1 iq2", "c1")
    ts(T.col[:, 4:5], T.iq[:, 1:2], 16.0, ALU.mult, "iq1", "c4", 15.0, ALU.add)
    ts(T.col[:, 5:6], T.iq[:, 0:1], 96.0, ALU.mult, "iq0", "c5")
    ts(T.col[:, 12:13], T.iq[:, 0:1], 6.0, ALU.mult, "iq0", "c12")
    ts(T.col[:, 13:14], T.iq[:, 3:4], 1530.0, ALU.mult, "iq3 c12", "c13", T.col[:, 12:13], ALU.add)
    C = [T.col[:, k:k + 1] for k in range(16)]
    ts(T.Ib[:], T.i144[:, 0:128], C[0], ALU.is_equal, "i144 c0", "Ib")
    for t in range(NT):
        ts(T.LX[:, 16 * t:16 * t + 16], T.il3[:], C[13], ALU.add, "il3 c13", "+LX", float(t), ALU.add)
    for k in range(16):
        act(T.E[:, k::16], T.Ib[:], ACT.Copy, "Ib", "+E")
    ts(T.W1[:], T.i144[:], C[4], ALU.is_equal, "i144 c4", "W1")
    ts(T.W2[:], T.i144[:], C[4], ALU.is_equal, "i144 c4", "W2", 2.0, ALU.mult)
    ts(T.Wn[:], T.i144[:], C[4], ALU.is_equal, "i144 c4", "Wn", -1.0, ALU.mult)
    ts(T.col[:, 6:7], T.iq[:, 0:1], 16.0, ALU.add, "iq0", "c6")
    ts(T.col[:, 7:8], T.iq[:, 0:1], 16.0, ALU.mult, "iq0", "c7")
    ts(T.col[:, 8:9], T.iq[:, 0:1], 0.0, ALU.is_equal, "iq0", "c8")
    ms(T.col[:, 9:10], 0.5, "HF")
    ms(T.col[:, 10:11], 0.5 - W, "HG")
    ms(T.col[:, 11:12], -1024.0, "HK")
    ms(T.col[:, 15:16], 1.0, "ONE")
    ts(T.BO[:], T.ig[:], C[2], ALU.is_equal, "ig c1", "BO")
    ts(T.t1[:], T.ik[:], C[1], ALU.is_equal, "ik c1", "t1")
    ts(T.t2[:], T.ik[:], 1.0, ALU.add, "ik c1", "t2", C[1], ALU.is_equal)
    ts(T.t4[:], T.ik[:], 2.0, ALU.add, "ik c1", "t4", C[1], ALU.is_equal)
    tt(T.DT[:], T.t1[:], T.t2[:], ALU.subtract, "t1 t2", "DT")
    tt(T.DU[:], T.t2[:], T.t4[:], ALU.subtract, "t2 t4", "DU")
    ms(T.MS[:], 1.0 / 16, "MS")
    tt(T.DT[:], T.DT[:], T.BO[:], ALU.mult, "DT BO", "DT")
    ts(T.DU[:, 14::16], T.DU[:, 14::16], C[8], ALU.subtract, "DU c8", "DU")
    ms(T.MS[:, 0::16], -BIG, "MS")
    ts(T.DU[:, 15::16], T.DU[:, 15::16], C[8], ALU.add, "DU c8", "DU")
    for t in range(NT):
        ts(T.LD[:, 18 * t:18 * t + 18], T.il[:], C[5], ALU.add, "il c5", "+LD", float(t), ALU.add)
    tt(T.DU[:], T.DU[:], T.BO[:], ALU.mult, "DU BO", "DU")
    ts(T.col[:, 14:15], T.iq[:, 4:5], 1.0 / 16, ALU.mult, "iq4", "c14")

    def late_constants():
        ts(T.MR[:], T.ia[:], C[1], ALU.is_lt, "ia c1", "MR", 8192.0, ALU.mult)
        ts(T.t3[:], T.ia[:], C[1], ALU.is_equal, "ia c1", "t3", -4096.0, ALU.mult)
        for c in range(2):
            rc = C[1] if c == 0 else C[6]
            ts(T.OFW[:, 33 * c:33 * c + 32], T.isw[:, 0:32], rc, ALU.is_ge, "isw c1 c6", "+OFW", 2.0, ALU.mult)
            ts(T.OFD[:, 129 * c + 32:129 * c + 128], T.isw[:, 32:128], rc, ALU.is_ge, "isw c1 c6", "+OFD", 2.0, ALU.mult)
            ts(T.OFD[:, 129 * c:129 * c + 32], T.isw[:, 0:32], rc, ALU.is_gt, "isw c1 c6", "+OFD", 2.0, ALU.mult)
        tt(T.MR[:], T.MR[:], T.t3[:], ALU.add, "MR t3", "MR")
        cp(T.OFW[:, 0:1], C[8], "c8", "OFW")
        ts(T.DM[:, 0:4], T.i144[:, 0:64:16], C[1], ALU.add, "i144 c1", "+DM", float(W), ALU.add)
        ts(T.DM[:, 4:6], T.i144[:, 0:32:16], C[1], ALU.add, "i144 c1", "+DM", 2.0 * W, ALU.add)
        ts(T.MR[:, 15::16], T.MR[:, 15::16], 4096.0 + W, ALU.add, "MR", "MR")
        tt(T.MD[:, 1:129], T.OFD[:, 1:129], T.OFD[:, 0:128], ALU.subtract, "OFD", "+MD")
        tt(T.MD[:, 130:258], T.OFD[:, 130:258], T.OFD[:, 129:257], ALU.subtract, "OFD", "+MD")
        ms(T.MD[:, 0:258:129], -BIG, "+MD")
        tt(T.MW[:, 1:33], T.OFW[:, 1:33], T.OFW[:, 0:32], ALU.subtract, "OFW", "+MW")
        tt(T.MW[:, 34:66], T.OFW[:, 34:66], T.OFW[:, 33:65], ALU.subtract, "OFW", "+MW")
        ms(T.MW[:, 0:66:33], -BIG, "+MW")
        ms(T.EQ[:, 128:258:129], 0.0, "EQp")
        ms(T.EW[:, 32:66:33], 0.0, "EWp")

    last_constants = [
        lambda: ts(T.BID[:, 0:4], T.il[:, 8:12], C[5], ALU.add, "il c5", "BID"),
        lambda: ts(T.MT[:], T.i144[:, 0:8], C[1], ALU.is_equal, "i144 c1", "MT"),
        lambda: ts(T.In[:], T.i144[:, 0:128], C[0], ALU.is_equal, "i144 c0", "In", -3072.0, ALU.mult),
        lambda: ts(T.CT[:], T.i144[:, 0:16], C[7], ALU.add, "i144 c7", "CT"),
        lambda: ts(T.MK[:], T.i144[:, 0:16], C[1], ALU.is_equal, "i144 c1", "MK"),
        lambda: ts(T.Wh[:], T.i144[:], C[4], ALU.is_equal, "i144 c4", "Wh"),
        lambda: ms(T.MM[:], -1.0 / 16, "MM"),
        lambda: cp(T.TG16[:], T.TG[:], "TG", "TG16"),
        lambda: ms(T.MM[:, 0::16], BIG, "MM"),
    ]

    def own_order(t):
        act(T.XO[:], T.X[:].indirect(T.LX[:, 16 * t:16 * t + 16]), ACT.Copy, "X LX", "XO")

    def spread(dst, src, e, r, w):
        for k in range(16):
            if e == "V":
                cp(dst[:, k::16], src, r, "+" + w)
            else:
                act(dst[:, k::16], src, ACT.Copy, r, "+" + w)

    def turn(src, r, k, sign=1.0):
        mm(T.PA[:, 0:128], src, T.Ib[:], True, True, r + " Ib", "PA")
        act(T.XT[:, 128 * k:128 * k + 128], T.PA[:, 0:128], ACT.Copy, "PA", "XT%d" % k, scale=sign)

    def bank(k, b, stop):
        mm(T["r%d" % b][:], T.XT[:, 128 * k:128 * k + 128], T.E[:, 512 * b:512 * b + 512], True, stop, "XT%d E" % k, "r%d" % b)

    def preload(k):
        for b in range(4):
            bank(k, b, True)

    def own_lists(t, h):
        for c in range(2):
            a = 1536 * c + 768 * h
            cp(OF[t][:, 128 * h + c:128 * h + 128:2], T.AQ[:, a + t:a + 768:ST], "AQ%d" % h, "+OF%d%d" % (t, h))

    def tables(t):
        X2, xn = (T.X3, "X3") if t == 2 else (T.X2, "X2")
        PT, pn = ((T.PA, "PA"), (T.D2, "D2"), (T.PB, "PB"))[t]
        DUP, dn = (T.DUQ, "DUQ") if t == 2 else (T.DUP, "DUP")

        def a():
            cp(DUP[:], T.AQ[:].indirect(T.LD[:, 18 * t:18 * t + 18]), AQ + " LD", dn)
            mm(PT[:, 0:272], T.DT[:], DUP[:, 0:272], True, True, "DT " + dn, pn)
            mm(PT[:, 272:400], T.DU[:], DUP[:, 0:128], True, True, "DU " + dn, pn)
            mm(PT[:, 400:416], T.DU[:], DUP[:, 0:16], True, True, "DU " + dn, pn)

        def d():
            act(T.DTU[:], X2[:].indirect(T.LH[:]), ACT.Copy, xn + " LH", "DTU")
        return [a, lambda: tr(X2[:, 0:256], PT[:, 0:256], pn, "+" + xn), lambda: tr(X2[:, 256:512], PT[:, 16:272], pn, "+" + xn),
                lambda: (tr(X2[:, 512:640], PT[:, 272:400], pn, "+" + xn), tr(X2[:, 640:768], PT[:, 288:416], pn, "+" + xn)), d]

    def pieces(own, t, XRb, xrr, D, dn, GA, ga_n, GB, gb_n):
        first = [True]
        off = OF[t] if own else T.AL
        ca = [64 * b if own else 32 * b for b in range(4)]
        cb = [64 * b + 32 if own else 128 + 32 * b for b in range(4)]
        offr = ["OF%d%d" % (t, b // 2) if own else "AL" for b in range(4)]

        def acc(wb, wn, q, rhs, r, last=False):
            mm(D[:, 0:256], wb[:, 15 - q:143 - q], rhs, first[0], last, wn + " " + r, dn)
            first[0] = False

        def halves(b):
            return [(0, 2)] if b < 3 else [(0, 1), (1, 2)]

        def ga(b):
            s = slice(512 * b, 512 * b + 512)
            tt(GA[:, s], T.X[:].indirect(off[:, ca[b]:ca[b] + 32]), XRb[:, s], ALU.subtract, "X %s %s" % (offr[b], xrr), ga_n + str(b))

        def gb(b):
            act(GB[:, 512 * b:512 * b + 512], T.X[:].indirect(off[:, cb[b]:cb[b] + 32]), ACT.Copy, "X " + offr[b], gb_n + str(b))

        def sumg(b):
            for h in range(2):
                acc(T.Wn, "Wn", cb[b] // 16 + h, GB[:, 512 * b + 256 * h:512 * b + 256 * h + 256], gb_n + str(b))

        def ab(b, only=None):
            for h0, h1 in halves(b) if only is None else [only]:
                s = slice(512 * b + 256 * h0, 512 * b + 256 * h1)
                act(T.AD[:, s], GA[:, s], ACT.Abs, ga_n + str(b), " ".join("AD%d%d" % (b, h) for h in range(h0, h1)))
                for h in range(h0, h1):
                    acc(T.W1, "W1", ca[b] // 16 + h, T.AD[:, 512 * b + 256 * h:512 * b + 256 * h + 256], "AD%d%d" % (b, h), only == (1, 2))

        def mx(b, only=None):
            for h0, h1 in halves(b) if only is None else [only]:
                s = slice(512 * b + 256 * h0, 512 * b + 256 * h1)
                tt(T.MX[:, s], GB[:, s], T["r%d" % b][:, 256 * h0:256 * h1], ALU.max, "%s%d r%d" % (gb_n, b, b),
                   " ".join("MX%d%d" % (b, h) for h in range(h0, h1)))
                for h in range(h0, h1):
                    acc(T.W2, "W2", cb[b] // 16 + h, T.MX[:, 512 * b + 256 * h:512 * b + 256 * h + 256], "MX%d%d" % (b, h))

        def df(b):
            bank(1, b, False)
            mm(T["r%d" % b][:], T.Ib[:], GB[:, 512 * b:512 * b + 512], False, True, "Ib %s%d" % (gb_n, b), "r%d" % b)

        def ac(b):
            act(T.MX[:, 512 * b:512 * b + 512], T["r%d" % b][:], ACT.Abs, "r%d" % b, "MX%d0 MX%d1" % (b, b))
            for h in range(2):
                acc(T.W1, "W1", cb[b] // 16 + h, T.MX[:, 512 * b + 256 * h:512 * b + 256 * h + 256], "MX%d%d" % (b, h), b == 3 and h == 1)

        def g8(j):
            G = GA if j < 4 else GB
            o, i = G[:, 512 * (j % 4):512 * (j % 4) + 512], T.XH[:].indirect(off[:, 32 * j:32 * j + 32])
            w = (ga_n if j < 4 else gb_n) + str(j % 4)
            if j in VJ:
                cp(o, i, "XH AL", w)
            else:
                act(o, i, ACT.Copy, "XH AL", w)

        def d8(j):
            G, b = (GA if j < 4 else GB), j % 4
            bank(1 + j // 4, b, False)
            mm(T["r%d" % b][:], T.Ib[:], G[:, 512 * b:512 * b + 512], False, True, "Ib %s%d" % (ga_n if j < 4 else gb_n, b), "r%d" % b)

        def a8(j):
            A, an, b = (T.AD, "AD", j) if j < 4 else (T.MX, "MX", j - 4)
            act(A[:, 512 * b:512 * b + 512], T["r%d" % b][:], ACT.Abs, "r%d" % b, "%s%d0 %s%d1" % (an, b, an, b))
            for h in range(2):
                acc(T.W1, "W1", 2 * j + h, A[:, 512 * b + 256 * h:512 * b + 256 * h + 256], "%s%d%d" % (an, b, h), j == 7 and h == 1)
        return ga, gb, sumg, ab, mx, df, ac, g8, d8, a8

    def distances(fs, hooks):
        ga, gb, sumg, ab, mx = fs[:5]
        steps = [(ga, 0), (gb, 0), (sumg, 0), (ga, 1), (gb, 1), (sumg, 1), (mx, 0), (ab, 0), (mx, 1), (gb, 2), (ga, 2), (sumg, 2), (ab, 1),
                 (mx, 2), (gb, 3), (ga, 3), (sumg, 3), (ab, 2), (lambda b: mx(b, (0, 1)), 3), (lambda b: ab(b, (0, 1)), 3),
                 (lambda b: mx(b, (1, 2)), 3), (lambda b: ab(b, (1, 2)), 3)]
        for n, (f, b) in enumerate(steps):
            f(b)
            for hk in hooks.get(n, []):
                hk()

    def nearest(t):
        def e():
            tt(T.MP[:], T.MK[:].indirect(T.KL[:]), T.ALT[:], ALU.mult, "MK KL ALT", "MP")
            for b in range(16):
                mm(T.PB[:, 0:16], T.Wh[:, 15 - b:143 - b], T.MP[:, 16 * b:16 * b + 16], b == 0, b == 15, "Wh MP", "PB")

        def f():
            ts(T.ML[:, 16 * t:16 * t + 16], T.PB[:, 0:16], 1024.0, ALU.add, "PB", "ML%d" % t)
            send(guest[t], "mm%d" % t, T.MI[:, 16 * t:16 * t + 16], T.ML[:, 16 * t:16 * t + 16], "ML%d" % t)
        return [lambda: scan(T.RM[:], T.MM[:], T.D2[:, 0:256], 0.0, ALU.add, ALU.min, "MM D2", "RM"),
                lambda: ts(T.k1[:], T.RM[:, 15::16], 16.0, ALU.mult, "RM", "k1", 15.0, ALU.add),
                lambda: ts(T.k2[:], T.k1[:], 15, ALU.bitwise_and, "k1", "k2"),
                lambda: cp(T.KL[:], T.k2[:], "k2", "KL"), e, f]

    def step(fill):
        if fill:
            f = fill.pop(0)
            if f is not None:
                f()

    def keep(t):
        tt(T.KP[:], T.AQ[:, t::ST], T.NF[:], ALU.mult, AQ + " NF", "KP")

    def learn(t, fill):
        tt(T.d1[:], T.ID[:].indirect(T.MI[:, 16 * t:16 * t + 16]), T.FM[:, L * t:L * t + L], ALU.mult, "ID MI%d FM%d" % (t, t), "d1")
        step(fill)
        if t + 1 < NT:
            tt(T.AQ[:, t::ST], T.d1[:], T.KP[:], ALU.add, "d1 KP", AQ)

    def told(t):
        y = T.YM[:, L * t:L * t + L]
        if t + 1 < NT:
            cp(y, T.AQ[:, t::ST], AQ, "YM%d" % t)
        else:
            tt(y, T.d1[:], T.KP[:], ALU.add, "d1 KP", "YM%d" % t)
        dma("Y", "om", T.ym[:, L * t:L * t + L], T.YM[t::16, L * t:L * t + L], "YM%d" % t, "ym%d" % t)

    def swap(t):
        return [lambda: cp(T.SW[:], T.SS[:].indirect(T.O6[:, 8 * t:8 * t + 4]), "SS O6%d O6b%d" % (t, t), "SW"),
                lambda: cp(T.SS[:].indirect(T.O6[:, 8 * t + 2:8 * t + 6]), T.SW[:], "SW O6%d" % t, "SS")]

    def targets(t, fill):
        u0 = 24 * t
        ut = "UT%d" % t
        scan(T.R[:, 0:32], T.MS[:, 0:32], T.D1[:, 0:32], 0.0, ALU.add, ALU.max, "MS D1", "R0")
        scan(T.R[:, 32:256], T.MS[:, 32:256], T.D1[:, 32:256], 0.0, ALU.add, ALU.max, "MS D1", "R1")
        tt(T.NR[:, 0:32], T.D1[:, 0:32], T.R[:, 0:32], ALU.not_equal, "D1 R0", "NR0")
        tt(T.NR[:, 32:128], T.D1[:, 32:128], T.R[:, 32:128], ALU.not_equal, "D1 R1", "NR1")
        scan(T.SC[:, 0:32], T.NR[:, 0:32], T.DTU[:, 256:288], 0.0, ALU.mult, ALU.add, "NR0 DTU", "SCu")
        scan(T.SC[:, 32:64], T.NR[:, 0:32], T.DTU[:, 0:32], 0.0, ALU.mult, ALU.add, "NR0 DTU", "SCt")
        tt(T.NR[:, 128:256], T.D1[:, 128:256], T.R[:, 128:256], ALU.not_equal, "D1 R1", "NR2")
        cp(T.OP[:], T.SC[:, 15:64:16], "SCu SCt", "OP")
        scan(T.SC[:, 64:160], T.NR[:, 32:128], T.DTU[:, 288:384], 0.0, ALU.mult, ALU.add, "NR1 DTU", "SCv")
        cp(T.RAW[:], T.SS[:].indirect(T.OP[:]), "SS OP", "RAW")
        scan(T.SC[:, 160:256], T.NR[:, 32:128], T.DTU[:, 32:128], 0.0, ALU.mult, ALU.add, "NR1 DTU", "SCw")
        for c in range(2):
            for j, a in enumerate((47, 15)):
                ts(T.EQ[:, 129 * c + 64 * j:129 * c + 64 * j + 64], T.RAW[:], T.SC[:, a + 16 * c:a + 16 * c + 1],
                   ALU.is_equal, "RAW SCu SCt", "EQ%d" % (2 * c + j))
        scan(T.SC[:, 256:384], T.NR[:, 128:256], T.DTU[:, 128:256], 0.0, ALU.mult, ALU.add, "NR2 DTU", "SCx")
        scan(T.FL[:, 0:258], T.MD[:, 0:258], T.EQ[:, 0:258], 0.0, ALU.add, ALU.max, "MD EQp EQ0 EQ1 EQ2 EQ3", "FL")
        cp(T.UT[:, u0 + 2:u0 + 22], T.SC[:, 79::16], "SCv SCw SCx", ut)
        step(fill)
        o0 = 8 * t
        for j, a in enumerate((47, 15)):
            for c in range(2):
                n = 2 * j + c
                ts(T.O6[:, o0 + 2 + n:o0 + 3 + n], T.FL[:, 129 * c + 128:129 * c + 129], T.DM[:, n:n + 1], ALU.mult,
                   "FL DM SCu SCt", "+O6%d" % t, T.SC[:, a + 16 * c:a + 16 * c + 1], ALU.max)
        step(fill)
        cp(T.SS[:].indirect(T.O6[:, o0 + 2:o0 + 6]), T.RAW[:], "RAW O6%d" % t, "SS")
        cp(T.O6[:, o0:o0 + 2], T.O6[:, o0 + 4:o0 + 6], "O6%d" % t, "O6b%d" % t)

        def lanes(r):
            at = T.UT[:, u0 + 6 + 2 * r:u0 + 8 + 2 * r] if r else T.OP[:, 2:4]
            cp(T.TT[:, W + ST * r + t:2 * W:96], T.SS[:].indirect(at), "SS OP " + ut, "TT%d" % r)
        lanes(1)
        rest = [lambda r=r: lanes(r) for r in (2, 3, 0, 4, 5, 6, 7)]
        rest.insert(0, lambda: cp(T.UR[:, 96 * t:96 * t + 96], T.SS[:].indirect(T.UT[:, u0 + 2:u0 + 8]), "SS " + ut, "UR%d" % t))
        allt = "TT0 TT1 TT2 TT3 TT4 TT5 TT6 TT7"

        def some(n):
            if not rest:
                step(fill)
            for _k in range(n):
                if rest:
                    rest.pop(0)()
        for w in range(1, 4):
            z = T.TT[:, W + ST * w + t:2 * W:96]
            ow = T.OW[:, 6 * t + 2 * w - 2:6 * t + 2 * w]
            some(2)
            scan(T.ZC[:], z, T.MR[:, 0:32], 1e5, ALU.min, ALU.add, "TT%d MR" % w, "ZC")
            some(2)
            for c in range(2):
                ts(T.EW[:, 33 * c:33 * c + 32], z, float(W), ALU.add, "TT%d ZC" % w, "EW%d" % c, T.ZC[:, 16 * c + 15:16 * c + 16], ALU.is_equal)
            some(2)
            scan(T.FW[:, 0:66], T.MW[:, 0:66], T.EW[:, 0:66], 0.0, ALU.add, ALU.max, "MW EWp EW0 EW1", "FW")
            some(2)
            for c in range(2):
                n = 6 * t + 2 * w - 2 + c
                ts(T.OW[:, n:n + 1], T.FW[:, 33 * c + 32:33 * c + 33], T.DM[:, 4 + c:5 + c], ALU.mult, "FW DM ZC", "+OW%d%d" % (t, w),
                   T.ZC[:, 16 * c + 15:16 * c + 16], ALU.max)
            if w == 1 and t + 1 < NT:
                cp(T.SS[:].indirect(T.O6[:, o0:o0 + 4]), T.RAW[:], "RAW O6%d O6b%d" % (t, t), "SS")
            else:
                step(fill)
            cp(T.TT[:].indirect(ow), T.UR[:, 96 * t + 32 * w - 32:96 * t + 32 * w], "UR%d OW%d%d" % (t, t, w), allt)
        step(fill)
        scan(T.AS[:], T.TT[:, W + t:2 * W:ST], T.MR[:], 1e5, ALU.min, ALU.add, allt + " MR", "AS")
        for j in range(2):
            cp(T.BT[:, 32 * j:32 * j + 32], T.TT[:, W + ST * (4 + j) + t:2 * W:96], allt, "BT%d" % j)
        ts(T.RQ[:, 16 * t:16 * t + 16], T.AS[:, 15::16], -float(W), ALU.add, "AS", "RQ%d" % t)
        send(host[t], "rq%d" % t, T.RI[:, 16 * t:16 * t + 16], T.RQ[:, 16 * t:16 * t + 16], "RQ%d" % t)

    def blockers(t, fill):
        while fill:
            step(fill)
        for j in range(4):
            ts(T.EB[:, 64 * j:64 * j + 64], T.BT[:], -float(t), ALU.add, "BT0 BT1 BID", "EB%d" % j, T.BID[:, j:j + 1], ALU.is_equal)
        scan(T.BC[:], T.BT[:], T.MR[:, 0:64], 1e5, ALU.min, ALU.add, "BT0 BT1 MR", "BC")
        scan(T.FB[:], T.MB[:], T.EB[:], 0.0, ALU.add, ALU.max, "MB EB0 EB1 EB2 EB3", "FB")
        for j in range(4):
            ts(T.EL[:, L * j:L * j + L], T.LID[:, L * t:L * t + L], T.BC[:, 16 * j + 15:16 * j + 16], ALU.is_equal, "LID BC FB", "EL%d" % j,
               T.FB[:, 64 * j + 63:64 * j + 64], ALU.is_gt)
            mm(T.PA[:, 0:256], T.BO[:], T.EL[:, L * j:L * j + L], j == 0, j == 3, "BO EL%d" % j, "PA")

    def freedom(t):
        act(T.Ab[:], T.PA[:, 0:256], ACT.Relu, "PA HF", "Ab", bias=C[9], scale=-1.0)
        act(T.D1[:, 0:256], T.PA[:, 0:256], ACT.Relu, "PA HF", "D1", bias=C[9], scale=-1.0)
        act(T.FM[:, L * t:L * t + L], T.PA[:, 0:256], ACT.Relu, "PA MT", "FM%d" % t, bias=T.MT[:, t:t + 1], scale=-1.0)
        act(T.NF[:], T.FM[:, L * t:L * t + L], ACT.Identity, "FM%d ONE" % t, "NF", bias=C[15], scale=-1.0)
        mm(T.PA[:, 256:512], T.Ib[:], T.XN[:, L * t:L * t + L], True, False, "Ib XN", "PA")
        mm(T.PA[:, 256:512], T.In[:], T.Ab[:], False, True, "In Ab", "PA")

    def scale(t):
        tt(T.Y[:], T.DI[:, L * t:L * t + L], T.D1[:, 0:256], ALU.mult, "DI%d D1" % t, "Y")

    def move(t):
        if t + 1 < NT:
            tt(T.X[:, t::ST], T.Y[:], T.PA[:, 256:512], ALU.add, "Y PA", "X")
        else:
            tt(T.YX[:, L * t:L * t + L], T.Y[:], T.PA[:, 256:512], ALU.add, "Y PA", "YX%d" % t)

    def alt():
        act(T.ALT[:], T.ALf[:].indirect(T.CT[:]), ACT.Identity, "ALf CT HK", "ALT", bias=C[11])

    def via(k):
        act(T.RR[:, L * k:L * k + L], T.SS[:].indirect(T.RQ[:, 16 * k:16 * k + 16]), ACT.Copy, "SS RQ%d" % k, "RR%d" % k)

    def viu(k):
        act(T.UR[:, 96 * k:96 * k + 96], T.SS[:].indirect(T.UT[:, 24 * k + 2:24 * k + 8]), ACT.Copy, "SS UT%d" % k, "UR%d" % k)

    def base():
        viu(0)
        act(T.YT[:, W:2 * W], T.SS[:].indirect(T.TG16[:]), ACT.Copy, "SS TG16", "YT")

    def alf():
        cp(T.ALf[:], T.AL[:], "AL", "ALf")

    own_order(0)
    late_constants()
    turn(T.XO[:, 128:256], "XO", 0)
    for t in range(NT):
        act(T.XN[:, L * t:L * t + L], T.X[:, t::ST], ACT.Copy, "X", "+XN")
    iota(T.il2[:, 0:16], [[32, 8], [256, 2]], 0, 0, "+il2")
    iota(T.il2[:, 16:24], [[32, 4], [128, 2]], 512, 0, "+il2")
    iota(T.ik[:, 0:16], [[0, 8], [-480, 2]], 224, 0, "ik")
    iota(T.ik[:, 16:24], [[0, 4], [-224, 2]], 96, 0, "ik2")
    iota(T.ik[:, 0:1], [[0, 1]], 480, 0, "ik")
    iota(T.ik[:, 16:17], [[0, 1]], 224, 0, "ik2")
    iota(T.SS[:], [[1, W + 64]], 0, 0, "SS", True)
    for t in range(NT):
        send(host[t], "xv%d" % t, T.XV[:, L * t:L * t + L], T.XN[:, L * t:L * t + L], "XN " + AQ)
    iota(T.MB[:], [[0, 256]], 0, 0, "MB", True)
    iota(T.MB[:, 0::64], [[0, 4]], -int(BIG), 0, "MB", True)
    iota(T.LID[:], [[1, NT], [ST, L]], W, 0, "LID", True)
    spread(T.XRo, T.XO[:, 0:128], "V", "XO", "XRo")
    preload(0)
    ts(T.t1[:, 0:24], T.ik[:, 0:24], C[14], ALU.mult, "ik ik2 c14 c1", "t1", C[3], ALU.add)
    own_lists(0, 0)
    tt(T.t2[:, 0:24], T.t1[:, 0:24], T.il2[:], ALU.add, "t1 il2", "t2")

    held = None
    tab = [tables(t) for t in range(NT)]
    for t in range(NT):
        if t == 0:
            a, b, c, d, e = tab[0]
            hooks = {0: [lambda: cp(T.LH[:], T.t2[:, 0:24], "t2", "LH")], 8: [lambda: own_lists(0, 1), a], 10: [b, c], 13: [d], 21: [e]}
        else:
            hooks = {}
        distances(pieces(True, t, T.XRo, "XRo", T.D1, "D1", T.GA, "GA", T.GB, "GB"), hooks)
        xv = "XV%d" % t
        if t == 0:
            dma("Y", "lh", T.XH[:], T.x[:], "DTU", "XH")
            tab[1][0]()
        if t == 1:
            alf()
        if t > 0:
            keep(t - 1)
        if t > 1:
            told(t - 2)
        if t == 1:
            g8, d8, a8 = held[7:10]
            for j in range(4):
                d8(j)
            for j in range(4):
                if 4 + j not in VJ:
                    g8(4 + j)
                a8(j)
                d8(4 + j)
            for j in range(4):
                a8(4 + j)
        if t == 2:
            ab, df, ac = held[3], held[5], held[6]
            for b in range(4):
                df(b)
                ab(b)
            for b in range(4):
                ac(b)
        if t > 0:
            alt()
        if t == 0:
            turn(T.XV[:, 0:128], xv, 1, -1.0)
            turn(T.XV[:, 128:256], xv, 2, -1.0)
        else:
            turn(T.XV[:, L * t + 128:L * t + 256], xv, 1, -1.0 if t + 1 < NT else 1.0)
        act(T.XF[:], T.XV[:, L * t:L * t + L], ACT.Identity, xv + " HG", "XF", bias=C[10])
        if t == 0:
            for k in range(1, NT):
                spread(XR[k], T.XV[:, L * k:L * k + 128], "S", "XV%d" % k, "XR%d" % k)
        if t + 1 < NT:
            own_order(t + 1)
            turn(T.XO[:, 128:256], "XO", 0)
            spread(T.XRo, T.XO[:, 0:128], "S", "XO", "XRo")
        if t == 0:
            fill = last_constants[:7] + [lambda: (own_lists(1, 0), own_lists(1, 1))] + tab[1][1:4] + last_constants[7:]
        elif t == 1:
            near = nearest(0)
            fill = [lambda: (own_lists(2, 0), own_lists(2, 1))] + tab[2][1:4] + [None] + near[:5] + [None, None, near[5]]
        else:
            preload(1)
            near = nearest(1)
            s1, s0 = swap(1), swap(0)
            fill = [None, None, lambda: via(1), s1[0], lambda: (s1[1](), via(0), viu(1)), near[0], near[1], s0[0],
                    lambda: (s0[1](), base()), near[2], near[3], near[4], None, near[5]]
        targets(t, fill)
        blockers(t, fill)
        if t == 0:
            tab[1][4]()
            tab[2][0]()
        if t == 1:
            tab[2][4]()
            act(T.YX[:, 0:L], T.X[:, 0::ST], ACT.Copy, "X", "YX0")
            dma("Y", "ox", T.yx[:, 0:L], T.YX[:, 0:L], "YX0", "yx0")
        if t + 1 < NT:
            freedom(t)
        ri = T.RI[:, 16 * t:16 * t + 16]

        def answer():
            tt(T.DD[:, L * t:L * t + L], T.X[:].indirect(ri), T.XF[:], ALU.subtract, "X XF RI%d" % t, "DD%d" % t)
            send(guest[t], "dd%d" % t, T.DI[:, L * t:L * t + L], T.DD[:, L * t:L * t + L], "DD%d" % t)
        if t == 0:
            answer()
        else:
            learn(t - 1, [])
        cp(T.AL[:], T.AQ[:].indirect(ri), AQ + " RI%d" % t, "AL")
        if t == 0:
            iota(T.ID[:], [[1, W]], 0, 0, "ID", True)
            held = pieces(False, t, None, "", T.D2, "D2", T.HA, "HA", T.HB, "HB")
            for j in range(4):
                held[7](j)
            preload(0)
            for j in VJ:
                held[7](j)
            scale(t)
            move(t)
        elif t == 1:
            answer()
            held = pieces(False, t, XR[t], "XR%d" % t, T.D2, "D2", T.HA, "HA", T.HB, "HB")
            preload(0)
            for b in range(4):
                held[0](b)
                held[1](b)
            scale(t)
            alf()
            move(t)
        else:
            distances(pieces(False, t, XR[t], "XR%d" % t, T.D2, "D2", T.GA, "GA", T.GB, "GB"), {0: [alf]})
            alt()
            freedom(t)
            answer()
            act(T.YX[:, L:2 * L], T.X[:, 1::ST], ACT.Copy, "X", "YX1")

    t = NT - 1
    near = nearest(t)
    merge = []
    for k in range(NT):
        for w in range(1, 4):
            merge.append(lambda k=k, w=w: cp(T.YT[:].indirect(T.OW[:, 6 * k + 2 * w - 2:6 * k + 2 * w]),
                                             T.UR[:, 96 * k + 32 * w - 32:96 * k + 32 * w], "UR%d OW%d%d" % (k, k, w), "YT"))
        if k + 1 < NT:
            merge.append(lambda k=k: act(T.YT[:, W + k:2 * W:ST], T.RR[:, L * k:L * k + L], ACT.Copy, "RR%d" % k, "YT"))
        else:
            merge.append(lambda k=k: (act(T.YT[:, W + k:2 * W:ST], T.TT[:, W + k:2 * W:ST], ACT.Copy, "TT0", "YT"),
                                      dma("Y", "ot", T.yt[:], T.YT[0::16, W:2 * W], "YT", "yt")))
    for f in near[0:5]:
        f()
    for _k in range(3):
        step(merge)
    near[5]()
    step(merge)
    told(1)
    for _k in range(4):
        step(merge)
    keep(t)
    step(merge)
    scale(t)
    step(merge)
    move(t)
    dma("Y", "ox", T.yx[:, L:3 * L], T.YX[:, L:3 * L], "YX1 YX2", "yx1")
    while len(merge) > 1:
        step(merge)
    learn(t, merge)
    told(t)
    for s in sorted(cnt):
        need("Y", (s, cnt[s]))
